import numpy as np
import ml_dtypes


def mxq(x, axis, fmt="e4m3"):
    dtype, down = {"e4m3": (ml_dtypes.float8_e4m3fn, 7), "e5m2": (ml_dtypes.float8_e5m2, 14)}[fmt]
    v = np.moveaxis(np.asarray(x, np.float32).astype(ml_dtypes.bfloat16).astype(np.float64), axis, -1)
    blocks = v.reshape(v.shape[:-1] + (-1, 32))
    amax = np.abs(blocks).max(-1, keepdims=True)
    byte = np.maximum(np.where(amax > 0, np.frexp(amax)[1] - 1 + 127, 0) - down, 1)
    scale = np.exp2(byte - 127.0)
    codes = (blocks / scale).astype(np.float32).astype(dtype).astype(np.float64)
    return np.moveaxis((codes * scale).reshape(v.shape), -1, axis)


WIDE = False


def mx_kscale(k):
    if not WIDE:
        return np.ones(k)
    levels = np.array([10, -10, 5, -5, 0])
    if k % 512:
        return np.exp2(np.random.permutation(np.resize(levels, k // 32))).repeat(32)
    a = np.empty((k // 512, 16))
    for p in range(k // 512):
        a[p, :8] = np.random.permutation(np.resize(levels, 8))
        for g in range(8):
            far = levels[np.abs(levels - a[p, g]) >= 10]
            a[p, g + 8] = far[np.random.randint(len(far))]
    return np.exp2(a.ravel()).repeat(32)


BF16 = ml_dtypes.bfloat16


def bf(x):
    return np.asarray(x, np.float32).astype(BF16)


def f64(x):
    return np.asarray(x).astype(np.float64)


E2M1 = np.array([0.0, 0.5, 1.0, 1.5, 2.0, 3.0, 4.0, 6.0, -0.0, -0.5, -1.0, -1.5, -2.0, -3.0, -4.0, -6.0])


def pack_weight(w, fmt):
    k, n = w.shape
    w = f64(bf(w)).reshape(k // 32, 32, n)
    amax = np.abs(w).max(1)
    if fmt == "e4m3":
        byte = np.frexp(amax)[1] - 1 + 127 - 7
    else:
        mant, ex = np.frexp(amax / 6.0)
        byte = np.where(mant > 0.5, ex, ex - 1) + 127
    byte = np.clip(np.where(amax > 0, byte, 1), 1, 254)
    scaled = (w * np.exp2(127.0 - byte)[:, None, :]).reshape(k, n).astype(np.float32)
    by_word = np.ascontiguousarray(scaled.reshape(k // 512, 128, 4, n).transpose(0, 1, 3, 2))
    if fmt == "e4m3":
        words = by_word.astype(ml_dtypes.float8_e4m3fn).view(np.uint8)
    else:
        c = by_word.astype(ml_dtypes.float4_e2m1fn).view(np.uint8) & 0xF
        words = c[..., 0::2] | (c[..., 1::2] << 4)
    return np.ascontiguousarray(words), np.ascontiguousarray(byte.astype(np.uint8).reshape(k // 512, 16, n))


def unpack_weight(words, scales, fmt):
    g, p, n, _ = words.shape
    if fmt == "e4m3":
        vals = np.ascontiguousarray(words).view(ml_dtypes.float8_e4m3fn).astype(np.float64)
    else:
        nib = np.empty((g, p, n, 4), np.uint8)
        nib[..., 0::2] = words & 0xF
        nib[..., 1::2] = words >> 4
        vals = E2M1[nib]
    vals = vals * np.repeat(np.exp2(scales.astype(np.float64) - 127.0), 8, axis=1)[..., None]
    return vals.transpose(0, 1, 3, 2).reshape(g * 512, n)
def pack4(w):
    words, scales = pack_weight(w, "e2m1")
    return words.reshape(words.shape[0], 128, -1), scales


def unpack4(words, scales):
    return unpack_weight(words.reshape(words.shape[0], 128, -1, 2), scales, "e2m1")


E4M3FN = np.array([(-1.0 if i & 128 else 1.0) * ((1.0 + (i & 7) / 8.0) * 2.0 ** (((i >> 3) & 15) - 7) if i & 120 else (i & 7) * 2.0 ** -9) for i in range(256)])


def e4m3fn_bytes(y):
    return np.clip(np.asarray(y, np.float64), -448.0, 448.0).astype(np.float32).astype(ml_dtypes.float8_e4m3fn).view(np.uint8)


def e4m3fn_values(b):
    return E4M3FN[b]


T, K, F, B = 512, 1024, 2048, 128


def setup_inputs():
    s, r = mx_kscale(K), mx_kscale(F)
    x = np.random.standard_normal((T, K)) * s
    wg = 1.5 * np.random.standard_normal((F, K)) / np.sqrt(K) / s
    wu = 1.5 * np.random.standard_normal((F, K)) / np.sqrt(K) / s
    smooth = (1 + 0.1 * np.random.standard_normal(F)) * r
    wd = np.random.standard_normal((F, K)) / np.sqrt(F) / r[:, None]
    xs = (np.abs(x).reshape(T, K // B, B).max(axis=2) / 448).astype(np.float32)
    gs = (np.abs(wg).reshape(F // B, B, K // B, B).max(axis=(1, 3)) / 448).astype(np.float32)
    us = (np.abs(wu).reshape(F // B, B, K // B, B).max(axis=(1, 3)) / 448).astype(np.float32)
    wd_words, wd_scales = pack4(wd)
    return {"x_bytes": e4m3fn_bytes(x / np.repeat(f64(xs), B, 1)), "x_scale": xs,
            "wg_bytes": e4m3fn_bytes(wg / np.repeat(np.repeat(f64(gs), B, 0), B, 1)), "wg_scale": gs,
            "wu_bytes": e4m3fn_bytes(wu / np.repeat(np.repeat(f64(us), B, 0), B, 1)), "wu_scale": us,
            "smooth": bf(smooth), "wd_words": wd_words, "wd_scales": wd_scales}


def reference(x_bytes, x_scale, wg_bytes, wg_scale, wu_bytes, wu_scale, smooth, wd_words, wd_scales):
    x = e4m3fn_values(x_bytes) * np.repeat(f64(x_scale), B, 1)
    wg = e4m3fn_values(wg_bytes) * np.repeat(np.repeat(f64(wg_scale), B, 0), B, 1)
    wu = e4m3fn_values(wu_bytes) * np.repeat(np.repeat(f64(wu_scale), B, 0), B, 1)
    xq = mxq(x, 1, "e4m3")
    a = xq @ mxq(wg, 1, "e4m3").T
    b = xq @ mxq(wu, 1, "e4m3").T
    h = a / (1 + np.exp(-a)) * b * f64(smooth)
    return mxq(h, 1, "e4m3") @ unpack4(wd_words, wd_scales)

@@ -1,0 +1,305 @@
+from contextlib import ExitStack
+
+import concourse.mybir as mybir
+from concourse.masks import make_identity
+
+T, K, F, N = 512, 1024, 2048, 1024
+FLOPS = 2 * T * K * 2 * F + 2 * T * F * N
+
+F32 = mybir.dt.float32
+BF16 = mybir.dt.bfloat16
+U32 = mybir.dt.uint32
+I32 = mybir.dt.int32
+U8 = mybir.dt.uint8
+FP8 = mybir.dt.float8_e4m3fn
+FP8X4 = mybir.dt.float8_e4m3fn_x4
+FP4X4 = mybir.dt.float4_e2m1fn_x4
+ACT = mybir.ActivationFunctionType
+ALU = mybir.AluOpType
+P = 128
+GROUPS = 4
+PAIRS = 16
+
+
+def tile_fp8_swiglu_smoothed_down_d4_kernel(tc, x_bytes, x_scale, wg_bytes, wg_scale, wu_bytes, wu_scale, smooth, wd_words, wd_scales, out):
+    nc = tc.nc
+    with ExitStack() as ctx:
+        keep = ctx.enter_context(tc.tile_pool(name="keep", bufs=1))
+        work = ctx.enter_context(tc.tile_pool(name="work", bufs=2))
+        psum = ctx.enter_context(tc.psum_pool(name="psum", bufs=1))
+
+        x_raw = [keep.tile([P, K], U8, name=f"x_raw{i}") for i in range(4)]
+        xv = x_bytes.rearrange("(p a) k -> p a k", a=4)
+        xs_col = keep.tile([P, 4, 8], F32, name="xs_col")
+        nc.scalar.dma_start(out=xs_col[:], in_=x_scale.rearrange("(p a) j -> p a j", a=4))
+        for i in range(4):
+            nc.sync.dma_start(out=x_raw[i][:], in_=xv[:, i, :])
+        w_spread = keep.tile([P, 2, P], F32, name="w_spread")
+        for w, sc in enumerate((wg_scale, wu_scale)):
+            nc.scalar.dma_start(out=w_spread[:, w, :], in_=sc.rearrange("i j -> (i j)").partition_broadcast(P))
+        sm_raw = keep.tile([P, GROUPS, 4], BF16, name="sm_raw")
+        nc.gpsimd.dma_start(out=sm_raw[:], in_=smooth.rearrange("(g p t) -> p g t", g=GROUPS, t=4))
+        w_raw = {}
+        wv = [b.rearrange("(g m t) k -> g m t k", g=GROUPS, t=4) for b in (wg_bytes, wu_bytes)]
+        for g in range(GROUPS):
+            for h in range(2):
+                for w in range(2):
+                    w_raw[(g, w, h)] = keep.tile([P, 2, K], U8, name=f"w_raw{g}{w}{h}")
+                    nc.sync.dma_start(out=w_raw[(g, w, h)][:], in_=wv[w][g][:, 2 * h : 2 * h + 2, :])
+        wd_codes = keep.tile([P, GROUPS, 2 * N], U8, align_bytes=64, name="wd_codes")
+        nc.sync.dma_start(out=wd_codes[:].bitcast(I32), in_=wd_words.bitcast(I32).rearrange("g p n -> p g n"))
+        wd_planes = keep.tile([P, GROUPS, N], U8, align_bytes=64, name="wd_planes")
+
+        ident = keep.tile([P, P], F32, name="ident")
+        make_identity(nc, ident[:])
+        w_cols = keep.tile([P, 2, GROUPS, 8], F32, name="w_cols")
+        def pick_cols(w, copy):
+            for q in range(4):
+                rows = slice(32 * q, 32 * q + 32)
+                copy(out=w_cols[rows, w, :, :], in_=w_spread[rows, w, :].rearrange("p (g q j) -> p g q j", g=GROUPS, q=4)[:, :, q, :])
+
+        pick_cols(1, nc.gpsimd.tensor_copy)
+        sm = keep.tile([P, GROUPS, 4], F32, name="sm")
+        nc.gpsimd.tensor_copy(out=sm[:], in_=sm_raw[:])
+        nc.gpsimd.memset(wd_planes[:].rearrange("p g n -> p (g n)").bitcast(I32), 0)
+        for q in range(4):
+            nc.sync.dma_start(out=wd_planes[32 * q : 32 * q + 4, :, :].bitcast(I32), in_=wd_scales.bitcast(I32).rearrange("g q n -> q g n")[4 * q : 4 * q + 4])
+
+        def widen_v(dst, src, cols, g):
+            for q in range(4):
+                o = dst[:, 512 * g : 512 * (g + 1)].rearrange("p (u w e) -> p w u e", u=2, e=2)[:, 32 * q : 32 * q + 32]
+                i = src[:, 512 * g + 128 * q : 512 * g + 128 * (q + 1)].bitcast(FP8).rearrange("p (w u e) -> p w u e", u=2, e=2)
+                nc.vector.tensor_scalar(out=o, in0=i, scalar1=cols[:, 4 * g + q : 4 * g + q + 1], scalar2=None, op0=ALU.mult)
+
+        def widen_s(dst, src, cols, g):
+            for q in range(4):
+                c = slice(512 * g + 128 * q, 512 * g + 128 * (q + 1))
+                nc.scalar.activation(out=dst[:, c], in_=src[:, c].bitcast(FP8), func=ACT.Copy, scale=cols[:, 4 * g + q : 4 * g + q + 1])
+
+        def transposes(bank, wide, on_s):
+            words = wide[:].bitcast(F32)
+            for g in range(2):
+                for u in range(2):
+                    if g in on_s:
+                        src = words[:, 256 * g + u : 256 * (g + 1) : 2]
+                    else:
+                        src = words[:, 256 * g + 128 * u : 256 * g + 128 * (u + 1)]
+                    nc.tensor.transpose(bank[:, g, u, :], src, ident[:])
+
+        def exit_copy(copy, dst, bank):
+            copy(out=dst, in_=bank[:].rearrange("p g u r -> p g r u"))
+
+        wide = {}
+        on_s = {}
+
+        def unit_src(i, w):
+            g, t = i // 4, i % 4
+            return w_raw[(g, w, t // 2)][:, t % 2, :], w_cols[:, w, g, :]
+
+        def alloc_wide(key, halves_on_s):
+            wide[key] = work.tile([P, K], BF16, tag="wide", bufs=8, name="wide_t")
+            on_s[key] = halves_on_s
+
+        def t_unit(key, tag):
+            bank = psum.tile([P, 2, 2, P], F32, tag=tag, name="bank_t")
+            transposes(bank, wide.pop(key), on_s[key])
+            return bank
+
+        xe = keep.tile([P, 2, T, 4], BF16, align_bytes=64, name="xe")
+        xq = keep.tile([P, 2, T], U32, align_bytes=64, name="xq")
+        xqs = keep.tile([P, 2, T], U8, align_bytes=64, name="xqs")
+        hq = [keep.tile([P, T], U32, align_bytes=64, name=f"hq{g}") for g in range(GROUPS)]
+        hqs = [keep.tile([P, T], U8, align_bytes=64, name=f"hqs{g}") for g in range(GROUPS)]
+
+        def x_unit_exit(a, bank, copy):
+            dst = xe[:, :, P * a : P * (a + 1), :].rearrange("p g r e -> p g (r e)").bitcast(F32).rearrange("p g (r u) -> p g r u", u=2)
+            exit_copy(copy, dst, bank)
+
+        def x_quant(g, h):
+            c = slice(256 * h, 256 * (h + 1))
+            nc.vector.quantize_mx(out=xq[:, g, c].bitcast(FP8X4), scales=xqs[:, g, c], in_=xe[:, g, c, :].rearrange("p r e -> p (r e)"))
+
+        def w_v(i, w, halves):
+            src, cols = unit_src(i, w)
+            for g in halves:
+                widen_v(wide[(i, w)], src, cols, g)
+
+        def w_s(i, w, halves):
+            src, cols = unit_src(i, w)
+            for g in halves:
+                widen_s(wide[(i, w)], src, cols, g)
+
+        S_COUNT = [2, 2] + [1] * 14
+
+        def s_halves(i, w):
+            return (1,) if w >= 2 - S_COUNT[i] else ()
+
+        def v_halves(i, w):
+            return tuple(g for g in range(2) if g not in s_halves(i, w))
+
+        ew, cw, cws, hm, sil, pa, pb = {}, {}, {}, {}, {}, {}, {}
+
+        def e_unit(i, w, copy, bank):
+            if i not in ew:
+                ew[i] = work.tile([P, 2, 2, P, 4], BF16, tag="ew", bufs=3, align_bytes=64, name="ew_t")
+            dst = ew[i][:, w].rearrange("p g r e -> p g (r e)").bitcast(F32).rearrange("p g (r u) -> p g r u", u=2)
+            exit_copy(copy, dst, bank)
+
+        def q_pair(i, parts):
+            if i not in cw:
+                cw[i] = work.tile([P, 2, 2, P], U32, tag="cw", bufs=3, align_bytes=64, name="cw_t")
+                cws[i] = work.tile([P, 2, 2, P], U8, tag="cws", bufs=3, align_bytes=64, name="cws_t")
+            for s in parts:
+                nc.vector.quantize_mx(
+                    out=cw[i][:, s].rearrange("p w g m -> p (w g m)").bitcast(FP8X4),
+                    scales=cws[i][:, s].rearrange("p w g m -> p (w g m)"),
+                    in_=ew[i][:, s].rearrange("p w g r e -> p (w g r e)"),
+                )
+
+        def m_pair(i):
+            pa[i] = psum.tile([P, T], F32, tag="a0", name="pa_t")
+            pb[i] = psum.tile([P, T], F32, tag="b0", name="pb_t")
+            for w, bank in ((0, pa[i]), (1, pb[i])):
+                for g in range(2):
+                    nc.tensor.matmul_mx(
+                        out=bank[:], lhsT=cw[i][:, w, g, :].bitcast(FP8X4), lhsT_scale=cws[i][:, w, g, :],
+                        rhs=xq[:, g, :].bitcast(FP8X4), rhs_scale=xqs[:, g, :], start=(g == 0), stop=(g == 1),
+                    )
+
+        def a_pair(i, cuts):
+            sil[i] = work.tile([P, T], F32, tag="sil", bufs=3, name="sil_t")
+            for c in cuts:
+                nc.scalar.activation(out=sil[i][:, c], in_=pa[i][:, c], func=ACT.Silu)
+
+        def b_pair(i, cuts):
+            g, t = i // 4, i % 4
+            if t == 0:
+                hm[g] = work.tile([P, 4, T], BF16, tag="hm", bufs=2, name="hm_t")
+            for c in cuts:
+                nc.vector.scalar_tensor_tensor(out=hm[g][:, t, c], in0=pb[i][:, c], scalar=sm[:, g, t : t + 1], in1=sil[i][:, c], op0=ALU.mult, op1=ALU.mult)
+
+        hi = {}
+
+        def i_chunk(g, c0, c1, copy):
+            if g not in hi:
+                hi[g] = work.tile([P, T, 4], BF16, tag="hi", bufs=2, align_bytes=64, name="hi_t")
+            dst = hi[g][:, c0:c1, :].rearrange("p (c i) t -> p c t i", i=4)
+            src = hm[g][:, :, c0:c1].rearrange("p t (c i) -> p c t i", i=4)
+            copy(out=dst, in_=src)
+
+        def qh_chunk(g, c0, c1):
+            nc.vector.quantize_mx(out=hq[g][:, c0:c1].bitcast(FP8X4), scales=hqs[g][:, c0:c1], in_=hi[g][:, c0:c1, :].rearrange("p r e -> p (r e)"))
+
+        ybank = {}
+
+        def y_alloc(a, tags):
+            for n in range(2):
+                ybank[(a, n)] = psum.tile([P, 512], F32, tag=tags[n], name="y_t")
+
+        def y_half(a, n, g):
+            nc.tensor.matmul_mx(
+                out=ybank[(a, n)][:], lhsT=hq[g][:, P * a : P * (a + 1)].bitcast(FP8X4), lhsT_scale=hqs[g][:, P * a : P * (a + 1)],
+                rhs=wd_codes[:, g, 1024 * n : 1024 * (n + 1)].bitcast(FP4X4), rhs_scale=wd_planes[:, g, 512 * n : 512 * (n + 1)],
+                start=(g == 0), stop=(g == 3),
+            )
+
+        def y_pass(a, g):
+            for n in range(2):
+                y_half(a, n, g)
+
+        ov = out.rearrange("(p a) n -> p a n", a=4)
+
+        def y_exit(a):
+            for n, copy in ((0, nc.scalar.copy), (1, nc.vector.tensor_copy)):
+                yt = work.tile([P, 512], F32, tag="yt", bufs=8, name="yt_t")
+                copy(out=yt[:], in_=ybank[(a, n)][:])
+                nc.sync.dma_start(out=ov[:, a, 512 * n : 512 * (n + 1)], in_=yt[:])
+
+        WHOLE = (slice(0, T),)
+        HALVES = (slice(0, 256), slice(256, 512))
+        BOTH = (slice(0, 2),)
+
+        with tc.manual_schedule(engines={mybir.EngineType.PE, mybir.EngineType.Activation, mybir.EngineType.DVE}):
+            for a in range(4):
+                alloc_wide(("x", a), (1,))
+            xcol = lambda a: xs_col[:, a, :]
+            for a in range(4):
+                widen_v(wide[("x", a)], x_raw[a], xcol(a), 0)
+                widen_s(wide[("x", a)], x_raw[a], xcol(a), 1)
+            pick_cols(0, nc.vector.tensor_copy)
+            xb = [t_unit(("x", a), ("t0", "t1", "a0", "b0")[a]) for a in range(4)]
+            for w in range(2):
+                alloc_wide((0, w), s_halves(0, w))
+            w_v(0, 0, v_halves(0, 0))
+            w_v(0, 1, v_halves(0, 1))
+            x_unit_exit(0, xb[0], nc.vector.tensor_copy)
+            x_unit_exit(1, xb[1], nc.vector.tensor_copy)
+            w_s(0, 0, s_halves(0, 0))
+            w_s(0, 1, s_halves(0, 1))
+            x_unit_exit(2, xb[2], nc.scalar.copy)
+            x_unit_exit(3, xb[3], nc.scalar.copy)
+            for w in range(2):
+                e_unit(0, w, nc.scalar.copy, t_unit((0, w), f"t{w}"))
+            for h in range(2):
+                for g in range(2):
+                    x_quant(g, h)
+            for w in range(2):
+                alloc_wide((1, w), s_halves(1, w))
+                w_s(1, w, s_halves(1, w))
+                w_v(1, w, v_halves(1, w))
+
+            y_alloc(0, ("y0", "y1"))
+            y_alloc(1, ("y2", "y3"))
+            LAST = PAIRS - 1
+            for s in range(PAIRS):
+                q_pair(s, BOTH if s < LAST else (slice(0, 1), slice(1, 2)))
+                if s + 2 < PAIRS:
+                    for w in range(2):
+                        alloc_wide((s + 2, w), s_halves(s + 2, w))
+                    w_v(s + 2, 0, v_halves(s + 2, 0)[:1])
+                if s + 1 < PAIRS:
+                    b0, b1 = (t_unit((s + 1, w), f"t{w}") for w in range(2))
+                    e_unit(s + 1, 0, nc.scalar.copy, b0)
+                    e_unit(s + 1, 1, nc.scalar.copy if s + 1 < LAST else nc.vector.tensor_copy, b1)
+                if s >= 1:
+                    b_pair(s - 1, WHOLE)
+                m_pair(s)
+                if s >= 7 and s % 4 == 3:
+                    qh_chunk(s // 4 - 1, 0, 512)
+                if s >= 8 and s % 4 < 2 and s < 14:
+                    y_pass(s % 4, s // 4 - 2)
+                if s + 2 < PAIRS:
+                    for w in range(2):
+                        w_s(s + 2, w, s_halves(s + 2, w))
+                if s >= 4:
+                    g, c = (s - 4) // 4, (s - 4) % 4
+                    if c < 2:
+                        i_chunk(g, P * 2 * c, P * (2 * c + 1), nc.scalar.copy)
+                        i_chunk(g, P * (2 * c + 1), P * (2 * c + 2), nc.vector.tensor_copy)
+                a_pair(s, WHOLE if s < LAST else HALVES)
+                if s + 2 < PAIRS:
+                    w_v(s + 2, 0, v_halves(s + 2, 0)[1:])
+                    w_v(s + 2, 1, v_halves(s + 2, 1))
+            y_alloc(2, ("t0", "t1"))
+            for g in range(2):
+                y_pass(2, g)
+            b_pair(LAST, HALVES)
+            for a in range(3):
+                y_pass(a, 2)
+            i_chunk(3, 0, 128, nc.vector.tensor_copy)
+            i_chunk(3, 128, 256, nc.scalar.copy)
+            i_chunk(3, 256, 384, nc.vector.tensor_copy)
+            qh_chunk(3, 0, 128)
+            y_pass(0, 3)
+            i_chunk(3, 384, 512, nc.scalar.copy)
+            qh_chunk(3, 128, 256)
+            y_pass(1, 3)
+            qh_chunk(3, 256, 384)
+            y_pass(2, 3)
+            qh_chunk(3, 384, 512)
+            y_alloc(3, ("a0", "b0"))
+            for n in range(2):
+                for g in range(4):
+                    y_half(3, n, g)
+            for a in range(4):
+                y_exit(a)

@@ -67,9 +67,8 @@ def tile_fp8_swiglu_smoothed_down_d4_kernel(tc, x_bytes, x_scale, wg_bytes, wg_s
 
         def widen_v(dst, src, cols, g):
             for q in range(4):
-                o = dst[:, 512 * g : 512 * (g + 1)].rearrange("p (u w e) -> p w u e", u=2, e=2)[:, 32 * q : 32 * q + 32]
-                i = src[:, 512 * g + 128 * q : 512 * g + 128 * (q + 1)].bitcast(FP8).rearrange("p (w u e) -> p w u e", u=2, e=2)
-                nc.vector.tensor_scalar(out=o, in0=i, scalar1=cols[:, 4 * g + q : 4 * g + q + 1], scalar2=None, op0=ALU.mult)
+                c = slice(512 * g + 128 * q, 512 * g + 128 * (q + 1))
+                nc.vector.tensor_scalar(out=dst[:, c], in0=src[:, c].bitcast(FP8), scalar1=cols[:, 4 * g + q : 4 * g + q + 1], scalar2=None, op0=ALU.mult)
 
         def widen_s(dst, src, cols, g):
             for q in range(4):
@@ -80,7 +79,7 @@ def tile_fp8_swiglu_smoothed_down_d4_kernel(tc, x_bytes, x_scale, wg_bytes, wg_s
             words = wide[:].bitcast(F32)
             for g in range(2):
                 for u in range(2):
-                    if g in on_s:
+                    if True:
                         src = words[:, 256 * g + u : 256 * (g + 1) : 2]
                     else:
                         src = words[:, 256 * g + 128 * u : 256 * g + 128 * (u + 1)]
@@ -156,10 +155,13 @@ def tile_fp8_swiglu_smoothed_down_d4_kernel(tc, x_bytes, x_scale, wg_bytes, wg_s
                     in_=ew[i][:, s].rearrange("p w g r e -> p (w g r e)"),
                 )
 
-        def m_pair(i):
+        def m_pair(i, between=()):
             pa[i] = psum.tile([P, T], F32, tag="a0", name="pa_t")
             pb[i] = psum.tile([P, T], F32, tag="b0", name="pb_t")
             for w, bank in ((0, pa[i]), (1, pb[i])):
+                if w == 1:
+                    for a, g in between:
+                        y_pass(a, g)
                 for g in range(2):
                     nc.tensor.matmul_mx(
                         out=bank[:], lhsT=cw[i][:, w, g, :].bitcast(FP8X4), lhsT_scale=cws[i][:, w, g, :],
@@ -253,6 +255,8 @@ def tile_fp8_swiglu_smoothed_down_d4_kernel(tc, x_bytes, x_scale, wg_bytes, wg_s
             LAST = PAIRS - 1
             for s in range(PAIRS):
                 q_pair(s, BOTH if s < LAST else (slice(0, 1), slice(1, 2)))
+                if s == 14:
+                    qh_chunk(2, 0, 512)
                 if s + 2 < PAIRS:
                     for w in range(2):
                         alloc_wide((s + 2, w), s_halves(s + 2, w))
@@ -263,8 +267,10 @@ def tile_fp8_swiglu_smoothed_down_d4_kernel(tc, x_bytes, x_scale, wg_bytes, wg_s
                     e_unit(s + 1, 1, nc.scalar.copy if s + 1 < LAST else nc.vector.tensor_copy, b1)
                 if s >= 1:
                     b_pair(s - 1, WHOLE)
-                m_pair(s)
-                if s >= 7 and s % 4 == 3:
+                if s == LAST:
+                    y_alloc(2, ("t0", "t1"))
+                m_pair(s, {14: ((0, 2),), 15: ((1, 2), (2, 0))}.get(s, ()))
+                if 7 <= s < 14 and s % 4 == 3:
                     qh_chunk(s // 4 - 1, 0, 512)
                 if s >= 8 and s % 4 < 2 and s < 14:
                     y_pass(s % 4, s // 4 - 2)
@@ -280,12 +286,9 @@ def tile_fp8_swiglu_smoothed_down_d4_kernel(tc, x_bytes, x_scale, wg_bytes, wg_s
                 if s + 2 < PAIRS:
                     w_v(s + 2, 0, v_halves(s + 2, 0)[1:])
                     w_v(s + 2, 1, v_halves(s + 2, 1))
-            y_alloc(2, ("t0", "t1"))
-            for g in range(2):
-                y_pass(2, g)
+            y_pass(2, 1)
+            y_pass(2, 2)
             b_pair(LAST, HALVES)
-            for a in range(3):
-                y_pass(a, 2)
             i_chunk(3, 0, 128, nc.vector.tensor_copy)
             i_chunk(3, 128, 256, nc.scalar.copy)
             i_chunk(3, 256, 384, nc.vector.tensor_copy)

@@ -28,37 +28,44 @@ def tile_fp8_swiglu_smoothed_down_d4_kernel(tc, x_bytes, x_scale, wg_bytes, wg_s
         work = ctx.enter_context(tc.tile_pool(name="work", bufs=2))
         psum = ctx.enter_context(tc.psum_pool(name="psum", bufs=1))
 
+        ident = keep.tile([P, P], F32, name="ident")
+        make_identity(nc, ident[:])
         x_raw = [keep.tile([P, K], U8, name=f"x_raw{i}") for i in range(4)]
         xv = x_bytes.rearrange("(p a) k -> p a k", a=4)
         xs_col = keep.tile([P, 4, 8], F32, name="xs_col")
         nc.scalar.dma_start(out=xs_col[:], in_=x_scale.rearrange("(p a) j -> p a j", a=4))
+        w_vec = keep.tile([P, 2], F32, name="w_vec")
+        w_vec2 = keep.tile([P, 8], F32, name="w_vec2")
+        nc.scalar.dma_start(out=w_vec[:, 0:1], in_=wg_scale.rearrange("i (j o) -> (i j) o", o=1))
+        nc.scalar.dma_start(out=w_vec2[:, 0:1], in_=wu_scale.rearrange("i (j o) -> (i j) o", o=1))
         for i in range(4):
             nc.sync.dma_start(out=x_raw[i][:], in_=xv[:, i, :])
-        w_spread = keep.tile([P, 2, P], F32, name="w_spread")
-        for w, sc in enumerate((wg_scale, wu_scale)):
-            nc.scalar.dma_start(out=w_spread[:, w, :], in_=sc.rearrange("i j -> (i j)").partition_broadcast(P))
-        sm_raw = keep.tile([P, GROUPS, 4], BF16, name="sm_raw")
-        nc.gpsimd.dma_start(out=sm_raw[:], in_=smooth.rearrange("(g p t) -> p g t", g=GROUPS, t=4))
         w_raw = {}
         wv = [b.rearrange("(g m t) k -> g m t k", g=GROUPS, t=4) for b in (wg_bytes, wu_bytes)]
+        sm_raw = keep.tile([P, GROUPS, 4], BF16, name="sm_raw")
         for g in range(GROUPS):
             for h in range(2):
                 for w in range(2):
                     w_raw[(g, w, h)] = keep.tile([P, 2, K], U8, name=f"w_raw{g}{w}{h}")
                     nc.sync.dma_start(out=w_raw[(g, w, h)][:], in_=wv[w][g][:, 2 * h : 2 * h + 2, :])
+            if g == 0:
+                nc.sync.dma_start(out=sm_raw[:], in_=smooth.rearrange("(g p t) -> p g t", g=GROUPS, t=4))
         wd_codes = keep.tile([P, GROUPS, 2 * N], U8, align_bytes=64, name="wd_codes")
         nc.sync.dma_start(out=wd_codes[:].bitcast(I32), in_=wd_words.bitcast(I32).rearrange("g p n -> p g n"))
         wd_planes = keep.tile([P, GROUPS, N], U8, align_bytes=64, name="wd_planes")
 
-        ident = keep.tile([P, P], F32, name="ident")
-        make_identity(nc, ident[:])
         w_cols = keep.tile([P, 2, GROUPS, 8], F32, name="w_cols")
+        w_spread = {}
+
+        def spread(w):
+            w_spread[w] = psum.tile([P, P], F32, tag=("y2", "y3")[w], name="w_spread")
+            v = (w_vec, w_vec2)[w][:, 0:1]
+            nc.tensor.matmul(w_spread[w][:], lhsT=v.to_broadcast([P, P]), rhs=ident[:], start=True, stop=True)
+
         def pick_cols(w, copy):
             for q in range(4):
                 rows = slice(32 * q, 32 * q + 32)
-                copy(out=w_cols[rows, w, :, :], in_=w_spread[rows, w, :].rearrange("p (g q j) -> p g q j", g=GROUPS, q=4)[:, :, q, :])
-
-        pick_cols(1, nc.gpsimd.tensor_copy)
+                copy(out=w_cols[rows, w, :, :], in_=w_spread[w][rows, :].rearrange("p (g q j) -> p g q j", g=GROUPS, q=4)[:, :, q, :])
         sm = keep.tile([P, GROUPS, 4], F32, name="sm")
         nc.gpsimd.tensor_copy(out=sm[:], in_=sm_raw[:])
         nc.gpsimd.memset(wd_planes[:].rearrange("p g n -> p (g n)").bitcast(I32), 0)
@@ -67,8 +74,9 @@ def tile_fp8_swiglu_smoothed_down_d4_kernel(tc, x_bytes, x_scale, wg_bytes, wg_s
 
         def widen_v(dst, src, cols, g):
             for q in range(4):
-                c = slice(512 * g + 128 * q, 512 * g + 128 * (q + 1))
-                nc.vector.tensor_scalar(out=dst[:, c], in0=src[:, c].bitcast(FP8), scalar1=cols[:, 4 * g + q : 4 * g + q + 1], scalar2=None, op0=ALU.mult)
+                o = dst[:, 512 * g : 512 * (g + 1)].rearrange("p (u w e) -> p w u e", u=2, e=2)[:, 32 * q : 32 * q + 32]
+                i = src[:, 512 * g + 128 * q : 512 * g + 128 * (q + 1)].bitcast(FP8).rearrange("p (w u e) -> p w u e", u=2, e=2)
+                nc.vector.tensor_scalar(out=o, in0=i, scalar1=cols[:, 4 * g + q : 4 * g + q + 1], scalar2=None, op0=ALU.mult)
 
         def widen_s(dst, src, cols, g):
             for q in range(4):
@@ -79,7 +87,7 @@ def tile_fp8_swiglu_smoothed_down_d4_kernel(tc, x_bytes, x_scale, wg_bytes, wg_s
             words = wide[:].bitcast(F32)
             for g in range(2):
                 for u in range(2):
-                    if True:
+                    if g in on_s:
                         src = words[:, 256 * g + u : 256 * (g + 1) : 2]
                     else:
                         src = words[:, 256 * g + 128 * u : 256 * g + 128 * (u + 1)]
@@ -225,10 +233,15 @@ def tile_fp8_swiglu_smoothed_down_d4_kernel(tc, x_bytes, x_scale, wg_bytes, wg_s
             for a in range(4):
                 alloc_wide(("x", a), (1,))
             xcol = lambda a: xs_col[:, a, :]
+            warm = keep.tile([P, 1], F32, name="warm")
+            nc.scalar.activation(out=warm[:], in_=ident[:, 0:1], func=ACT.Silu)
+            spread(0)
+            spread(1)
             for a in range(4):
                 widen_v(wide[("x", a)], x_raw[a], xcol(a), 0)
                 widen_s(wide[("x", a)], x_raw[a], xcol(a), 1)
             pick_cols(0, nc.vector.tensor_copy)
+            pick_cols(1, nc.vector.tensor_copy)
             xb = [t_unit(("x", a), ("t0", "t1", "a0", "b0")[a]) for a in range(4)]
             for w in range(2):
                 alloc_wide((0, w), s_halves(0, w))
@@ -269,7 +282,7 @@ def tile_fp8_swiglu_smoothed_down_d4_kernel(tc, x_bytes, x_scale, wg_bytes, wg_s
                     b_pair(s - 1, WHOLE)
                 if s == LAST:
                     y_alloc(2, ("t0", "t1"))
-                m_pair(s, {14: ((0, 2),), 15: ((1, 2), (2, 0))}.get(s, ()))
+                m_pair(s, {14: ((0, 2),), 15: ((1, 2),)}.get(s, ()))
                 if 7 <= s < 14 and s % 4 == 3:
                     qh_chunk(s // 4 - 1, 0, 512)
                 if s >= 8 and s % 4 < 2 and s < 14:
@@ -286,9 +299,11 @@ def tile_fp8_swiglu_smoothed_down_d4_kernel(tc, x_bytes, x_scale, wg_bytes, wg_s
                 if s + 2 < PAIRS:
                     w_v(s + 2, 0, v_halves(s + 2, 0)[1:])
                     w_v(s + 2, 1, v_halves(s + 2, 1))
-            y_pass(2, 1)
-            y_pass(2, 2)
+            for g in range(3):
+                y_pass(2, g)
             b_pair(LAST, HALVES)
+            y_alloc(3, ("a0", "b0"))
+            y_pass(3, 0)
             i_chunk(3, 0, 128, nc.vector.tensor_copy)
             i_chunk(3, 128, 256, nc.scalar.copy)
             i_chunk(3, 256, 384, nc.vector.tensor_copy)
@@ -300,9 +315,7 @@ def tile_fp8_swiglu_smoothed_down_d4_kernel(tc, x_bytes, x_scale, wg_bytes, wg_s
             qh_chunk(3, 256, 384)
             y_pass(2, 3)
             qh_chunk(3, 384, 512)
-            y_alloc(3, ("a0", "b0"))
-            for n in range(2):
-                for g in range(4):
-                    y_half(3, n, g)
+            for g in range(1, 4):
+                y_pass(3, g)
             for a in range(4):
                 y_exit(a)

@@ -18,6 +18,9 @@ ACT = mybir.ActivationFunctionType
 ALU = mybir.AluOpType
 P = 128
 GROUPS = 4
+ORDER = ["Q","T0","Wa","QH","T1","Y","Sa","E0","B","E1","Wb","Ma","IS","Mb","Sb","Wc","A","IV"]
+NA, NB, NSA = 3, 4, 3
+SCOUNT = [2] + [1] * 15
 PAIRS = 16
 
 
@@ -30,6 +33,8 @@ def tile_fp8_swiglu_smoothed_down_d4_kernel(tc, x_bytes, x_scale, wg_bytes, wg_s
 
         ident = keep.tile([P, P], F32, name="ident")
         make_identity(nc, ident[:])
+        wd_planes = keep.tile([P, GROUPS, N], U8, align_bytes=64, name="wd_planes")
+        nc.gpsimd.memset(wd_planes[:].rearrange("p g n -> p (g n)").bitcast(I32), 0)
         x_raw = [keep.tile([P, K], U8, name=f"x_raw{i}") for i in range(4)]
         xv = x_bytes.rearrange("(p a) k -> p a k", a=4)
         xs_col = keep.tile([P, 4, 8], F32, name="xs_col")
@@ -48,38 +53,37 @@ def tile_fp8_swiglu_smoothed_down_d4_kernel(tc, x_bytes, x_scale, wg_bytes, wg_s
                 for w in range(2):
                     w_raw[(g, w, h)] = keep.tile([P, 2, K], U8, name=f"w_raw{g}{w}{h}")
                     nc.sync.dma_start(out=w_raw[(g, w, h)][:], in_=wv[w][g][:, 2 * h : 2 * h + 2, :])
-            if g == 0:
+            if g == 1:
                 nc.sync.dma_start(out=sm_raw[:], in_=smooth.rearrange("(g p t) -> p g t", g=GROUPS, t=4))
         wd_codes = keep.tile([P, GROUPS, 2 * N], U8, align_bytes=64, name="wd_codes")
         nc.sync.dma_start(out=wd_codes[:].bitcast(I32), in_=wd_words.bitcast(I32).rearrange("g p n -> p g n"))
-        wd_planes = keep.tile([P, GROUPS, N], U8, align_bytes=64, name="wd_planes")
 
         w_cols = keep.tile([P, 2, GROUPS, 8], F32, name="w_cols")
         w_spread = {}
 
         def spread(w):
-            w_spread[w] = psum.tile([P, P], F32, tag=("y2", "y3")[w], name="w_spread")
+            if w == 0:
+                w_spread[0] = psum.tile([P, 2, P], F32, tag="y2", name="w_spread")
             v = (w_vec, w_vec2)[w][:, 0:1]
-            nc.tensor.matmul(w_spread[w][:], lhsT=v.to_broadcast([P, P]), rhs=ident[:], start=True, stop=True)
+            nc.tensor.matmul(w_spread[0][:, w, :], lhsT=v.to_broadcast([P, P]), rhs=ident[:], start=True, stop=True)
 
-        def pick_cols(w, copy):
+        def pick_cols(copy):
             for q in range(4):
                 rows = slice(32 * q, 32 * q + 32)
-                copy(out=w_cols[rows, w, :, :], in_=w_spread[w][rows, :].rearrange("p (g q j) -> p g q j", g=GROUPS, q=4)[:, :, q, :])
+                copy(out=w_cols[rows, :, :, :], in_=w_spread[0][rows, :, :].rearrange("p w (g q j) -> p w g q j", g=GROUPS, q=4)[:, :, :, q, :])
         sm = keep.tile([P, GROUPS, 4], F32, name="sm")
         nc.gpsimd.tensor_copy(out=sm[:], in_=sm_raw[:])
-        nc.gpsimd.memset(wd_planes[:].rearrange("p g n -> p (g n)").bitcast(I32), 0)
         for q in range(4):
             nc.sync.dma_start(out=wd_planes[32 * q : 32 * q + 4, :, :].bitcast(I32), in_=wd_scales.bitcast(I32).rearrange("g q n -> q g n")[4 * q : 4 * q + 4])
 
-        def widen_v(dst, src, cols, g):
-            for q in range(4):
+        def widen_v(dst, src, cols, g, blocks=(0, 1, 2, 3)):
+            for q in blocks:
                 o = dst[:, 512 * g : 512 * (g + 1)].rearrange("p (u w e) -> p w u e", u=2, e=2)[:, 32 * q : 32 * q + 32]
                 i = src[:, 512 * g + 128 * q : 512 * g + 128 * (q + 1)].bitcast(FP8).rearrange("p (w u e) -> p w u e", u=2, e=2)
                 nc.vector.tensor_scalar(out=o, in0=i, scalar1=cols[:, 4 * g + q : 4 * g + q + 1], scalar2=None, op0=ALU.mult)
 
-        def widen_s(dst, src, cols, g):
-            for q in range(4):
+        def widen_s(dst, src, cols, g, blocks=(0, 1, 2, 3)):
+            for q in blocks:
                 c = slice(512 * g + 128 * q, 512 * g + 128 * (q + 1))
                 nc.scalar.activation(out=dst[:, c], in_=src[:, c].bitcast(FP8), func=ACT.Copy, scale=cols[:, 4 * g + q : 4 * g + q + 1])
 
@@ -136,7 +140,7 @@ def tile_fp8_swiglu_smoothed_down_d4_kernel(tc, x_bytes, x_scale, wg_bytes, wg_s
             for g in halves:
                 widen_s(wide[(i, w)], src, cols, g)
 
-        S_COUNT = [2, 2] + [1] * 14
+        S_COUNT = SCOUNT
 
         def s_halves(i, w):
             return (1,) if w >= 2 - S_COUNT[i] else ()
@@ -163,18 +167,13 @@ def tile_fp8_swiglu_smoothed_down_d4_kernel(tc, x_bytes, x_scale, wg_bytes, wg_s
                     in_=ew[i][:, s].rearrange("p w g r e -> p (w g r e)"),
                 )
 
-        def m_pair(i, between=()):
-            pa[i] = psum.tile([P, T], F32, tag="a0", name="pa_t")
-            pb[i] = psum.tile([P, T], F32, tag="b0", name="pb_t")
-            for w, bank in ((0, pa[i]), (1, pb[i])):
-                if w == 1:
-                    for a, g in between:
-                        y_pass(a, g)
-                for g in range(2):
-                    nc.tensor.matmul_mx(
-                        out=bank[:], lhsT=cw[i][:, w, g, :].bitcast(FP8X4), lhsT_scale=cws[i][:, w, g, :],
-                        rhs=xq[:, g, :].bitcast(FP8X4), rhs_scale=xqs[:, g, :], start=(g == 0), stop=(g == 1),
-                    )
+        def m_half(i, w):
+            (pa, pb)[w][i] = psum.tile([P, T], F32, tag=("a0", "b0")[w], name="pm_t")
+            for g in range(2):
+                nc.tensor.matmul_mx(
+                    out=(pa, pb)[w][i][:], lhsT=cw[i][:, w, g, :].bitcast(FP8X4), lhsT_scale=cws[i][:, w, g, :],
+                    rhs=xq[:, g, :].bitcast(FP8X4), rhs_scale=xqs[:, g, :], start=(g == 0), stop=(g == 1),
+                )
 
         def a_pair(i, cuts):
             sil[i] = work.tile([P, T], F32, tag="sil", bufs=3, name="sil_t")
@@ -225,6 +224,13 @@ def tile_fp8_swiglu_smoothed_down_d4_kernel(tc, x_bytes, x_scale, wg_bytes, wg_s
                 copy(out=yt[:], in_=ybank[(a, n)][:])
                 nc.sync.dma_start(out=ov[:, a, 512 * n : 512 * (n + 1)], in_=yt[:])
 
+        def y_exit_last():
+            for n in range(2):
+                for h, copy in ((0, nc.scalar.copy), (1, nc.vector.tensor_copy)):
+                    yt = work.tile([P, 256], F32, tag="yl", bufs=4, name="yl_t")
+                    copy(out=yt[:], in_=ybank[(3, n)][:, 256 * h : 256 * (h + 1)])
+                    nc.sync.dma_start(out=ov[:, 3, 512 * n + 256 * h : 512 * n + 256 * (h + 1)], in_=yt[:])
+
         WHOLE = (slice(0, T),)
         HALVES = (slice(0, 256), slice(256, 512))
         BOTH = (slice(0, 2),)
@@ -240,8 +246,7 @@ def tile_fp8_swiglu_smoothed_down_d4_kernel(tc, x_bytes, x_scale, wg_bytes, wg_s
             for a in range(4):
                 widen_v(wide[("x", a)], x_raw[a], xcol(a), 0)
                 widen_s(wide[("x", a)], x_raw[a], xcol(a), 1)
-            pick_cols(0, nc.vector.tensor_copy)
-            pick_cols(1, nc.vector.tensor_copy)
+            pick_cols(nc.vector.tensor_copy)
             xb = [t_unit(("x", a), ("t0", "t1", "a0", "b0")[a]) for a in range(4)]
             for w in range(2):
                 alloc_wide((0, w), s_halves(0, w))
@@ -266,39 +271,84 @@ def tile_fp8_swiglu_smoothed_down_d4_kernel(tc, x_bytes, x_scale, wg_bytes, wg_s
             y_alloc(0, ("y0", "y1"))
             y_alloc(1, ("y2", "y3"))
             LAST = PAIRS - 1
-            for s in range(PAIRS):
+            banks = {}
+
+            def op_q(s):
                 q_pair(s, BOTH if s < LAST else (slice(0, 1), slice(1, 2)))
-                if s == 14:
-                    qh_chunk(2, 0, 512)
+
+            def v_list(i):
+                return [(w, g, b) for w in range(2) for g in v_halves(i, w) for b in range(4)]
+
+            def s_list(i):
+                return [(w, g, b) for w in range(2) for g in s_halves(i, w) for b in range(4)]
+
+            def op_w(s, lo, hi):
+                if s + 2 < PAIRS:
+                    for w, g, b in v_list(s + 2)[lo:hi]:
+                        src, cols = unit_src(s + 2, w)
+                        widen_v(wide[(s + 2, w)], src, cols, g, (b,))
+
+            def op_ws(s, lo, hi):
+                if s + 2 < PAIRS:
+                    for w, g, b in s_list(s + 2)[lo:hi]:
+                        src, cols = unit_src(s + 2, w)
+                        widen_s(wide[(s + 2, w)], src, cols, g, (b,))
+
+            def op_alloc(s):
                 if s + 2 < PAIRS:
                     for w in range(2):
                         alloc_wide((s + 2, w), s_halves(s + 2, w))
-                    w_v(s + 2, 0, v_halves(s + 2, 0)[:1])
+
+            def op_t(s, w):
                 if s + 1 < PAIRS:
-                    b0, b1 = (t_unit((s + 1, w), f"t{w}") for w in range(2))
-                    e_unit(s + 1, 0, nc.scalar.copy, b0)
-                    e_unit(s + 1, 1, nc.scalar.copy if s + 1 < LAST else nc.vector.tensor_copy, b1)
+                    banks[w] = t_unit((s + 1, w), f"t{w}")
+
+            def op_e(s, w):
+                if s + 1 < PAIRS:
+                    e_unit(s + 1, w, nc.vector.tensor_copy if w == 1 and s + 1 == LAST else nc.scalar.copy, banks[w])
+
+            def op_b(s):
                 if s >= 1:
                     b_pair(s - 1, WHOLE)
-                if s == LAST:
-                    y_alloc(2, ("t0", "t1"))
-                m_pair(s, {14: ((0, 2),), 15: ((1, 2),)}.get(s, ()))
-                if 7 <= s < 14 and s % 4 == 3:
-                    qh_chunk(s // 4 - 1, 0, 512)
-                if s >= 8 and s % 4 < 2 and s < 14:
-                    y_pass(s % 4, s // 4 - 2)
-                if s + 2 < PAIRS:
-                    for w in range(2):
-                        w_s(s + 2, w, s_halves(s + 2, w))
+
+            def op_m(s, w):
+                m_half(s, w)
+
+            def op_i(s, v):
                 if s >= 4:
                     g, c = (s - 4) // 4, (s - 4) % 4
                     if c < 2:
-                        i_chunk(g, P * 2 * c, P * (2 * c + 1), nc.scalar.copy)
-                        i_chunk(g, P * (2 * c + 1), P * (2 * c + 2), nc.vector.tensor_copy)
+                        k = 2 * c + v
+                        i_chunk(g, P * k, P * (k + 1), nc.vector.tensor_copy if v else nc.scalar.copy)
+
+            def op_qh(s):
+                if 7 <= s < 14 and s % 4 == 3:
+                    qh_chunk(s // 4 - 1, 0, 512)
+                if s == 14:
+                    qh_chunk(2, 0, 512)
+
+            def op_y(s):
+                if s >= 8 and s % 4 < 2 and s < 14:
+                    y_pass(s % 4, s // 4 - 2)
+                if s == LAST:
+                    y_pass(0, 2)
+
+            def op_a(s):
                 a_pair(s, WHOLE if s < LAST else HALVES)
-                if s + 2 < PAIRS:
-                    w_v(s + 2, 0, v_halves(s + 2, 0)[1:])
-                    w_v(s + 2, 1, v_halves(s + 2, 1))
+
+            OPS = {
+                "Q": op_q, "Wa": lambda s: op_w(s, 0, NA), "Wb": lambda s: op_w(s, NA, NB), "Wc": lambda s: op_w(s, NB, 16),
+                "Sa": lambda s: op_ws(s, 0, NSA), "Sb": lambda s: op_ws(s, NSA, 16),
+                "T0": lambda s: op_t(s, 0), "T1": lambda s: op_t(s, 1), "E0": lambda s: op_e(s, 0), "E1": lambda s: op_e(s, 1),
+                "B": op_b, "Ma": lambda s: op_m(s, 0), "Mb": lambda s: op_m(s, 1), "IS": lambda s: op_i(s, 0), "IV": lambda s: op_i(s, 1),
+                "QH": op_qh, "Y": op_y, "A": op_a,
+            }
+            for s in range(PAIRS):
+                op_alloc(s)
+                for o in ORDER:
+                    OPS[o](s)
+            y_alloc(2, ("t0", "t1"))
+            y_pass(1, 2)
             for g in range(3):
                 y_pass(2, g)
             b_pair(LAST, HALVES)
@@ -315,7 +365,9 @@ def tile_fp8_swiglu_smoothed_down_d4_kernel(tc, x_bytes, x_scale, wg_bytes, wg_s
             qh_chunk(3, 256, 384)
             y_pass(2, 3)
             qh_chunk(3, 384, 512)
-            for g in range(1, 4):
-                y_pass(3, g)
-            for a in range(4):
+            for n in range(2):
+                for g in range(1, 4):
+                    y_half(3, n, g)
+            for a in range(3):
                 y_exit(a)
+            y_exit_last()

from contextlib import ExitStack

import concourse.mybir as mybir
from concourse.masks import make_identity

T, K, F, N = 512, 1024, 2048, 1024
FLOPS = 2 * T * K * 2 * F + 2 * T * F * N

F32 = mybir.dt.float32
BF16 = mybir.dt.bfloat16
U32 = mybir.dt.uint32
I32 = mybir.dt.int32
U8 = mybir.dt.uint8
FP8 = mybir.dt.float8_e4m3fn
FP8X4 = mybir.dt.float8_e4m3fn_x4
FP4X4 = mybir.dt.float4_e2m1fn_x4
ACT = mybir.ActivationFunctionType
ALU = mybir.AluOpType
P = 128
GROUPS = 4
ORDER = ["Q","T0","Wa","QH","T1","Y","Sa","E0","B","E1","Wb","Ma","IS","Mb","Sb","Wc","A","IV"]
NA, NB, NSA = 3, 4, 3
SCOUNT = [2] + [1] * 15
PAIRS = 16


def tile_fp8_swiglu_smoothed_down_d4_kernel(tc, x_bytes, x_scale, wg_bytes, wg_scale, wu_bytes, wu_scale, smooth, wd_words, wd_scales, out):
    nc = tc.nc
    with ExitStack() as ctx:
        keep = ctx.enter_context(tc.tile_pool(name="keep", bufs=1))
        work = ctx.enter_context(tc.tile_pool(name="work", bufs=2))
        psum = ctx.enter_context(tc.psum_pool(name="psum", bufs=1))

        ident = keep.tile([P, P], F32, name="ident")
        make_identity(nc, ident[:])
        wd_planes = keep.tile([P, GROUPS, N], U8, align_bytes=64, name="wd_planes")
        nc.gpsimd.memset(wd_planes[:].rearrange("p g n -> p (g n)").bitcast(I32), 0)
        x_raw = [keep.tile([P, K], U8, name=f"x_raw{i}") for i in range(4)]
        xv = x_bytes.rearrange("(p a) k -> p a k", a=4)
        xs_col = keep.tile([P, 4, 8], F32, name="xs_col")
        nc.scalar.dma_start(out=xs_col[:], in_=x_scale.rearrange("(p a) j -> p a j", a=4))
        w_vec = keep.tile([P, 2], F32, name="w_vec")
        w_vec2 = keep.tile([P, 8], F32, name="w_vec2")
        nc.scalar.dma_start(out=w_vec[:, 0:1], in_=wg_scale.rearrange("i (j o) -> (i j) o", o=1))
        nc.scalar.dma_start(out=w_vec2[:, 0:1], in_=wu_scale.rearrange("i (j o) -> (i j) o", o=1))
        for i in range(4):
            nc.sync.dma_start(out=x_raw[i][:], in_=xv[:, i, :])
        w_raw = {}
        wv = [b.rearrange("(g m t) k -> g m t k", g=GROUPS, t=4) for b in (wg_bytes, wu_bytes)]
        sm_raw = keep.tile([P, GROUPS, 4], BF16, name="sm_raw")
        for g in range(GROUPS):
            for h in range(2):
                for w in range(2):
                    w_raw[(g, w, h)] = keep.tile([P, 2, K], U8, name=f"w_raw{g}{w}{h}")
                    nc.sync.dma_start(out=w_raw[(g, w, h)][:], in_=wv[w][g][:, 2 * h : 2 * h + 2, :])
            if g == 1:
                nc.sync.dma_start(out=sm_raw[:], in_=smooth.rearrange("(g p t) -> p g t", g=GROUPS, t=4))
        wd_codes = keep.tile([P, GROUPS, 2 * N], U8, align_bytes=64, name="wd_codes")
        nc.sync.dma_start(out=wd_codes[:].bitcast(I32), in_=wd_words.bitcast(I32).rearrange("g p n -> p g n"))

        w_cols = keep.tile([P, 2, GROUPS, 8], F32, name="w_cols")
        w_spread = {}

        def spread(w):
            if w == 0:
                w_spread[0] = psum.tile([P, 2, P], F32, tag="y2", name="w_spread")
            v = (w_vec, w_vec2)[w][:, 0:1]
            nc.tensor.matmul(w_spread[0][:, w, :], lhsT=v.to_broadcast([P, P]), rhs=ident[:], start=True, stop=True)

        def pick_cols(copy):
            for q in range(4):
                rows = slice(32 * q, 32 * q + 32)
                copy(out=w_cols[rows, :, :, :], in_=w_spread[0][rows, :, :].rearrange("p w (g q j) -> p w g q j", g=GROUPS, q=4)[:, :, :, q, :])
        sm = keep.tile([P, GROUPS, 4], F32, name="sm")
        nc.gpsimd.tensor_copy(out=sm[:], in_=sm_raw[:])
        for q in range(4):
            nc.sync.dma_start(out=wd_planes[32 * q : 32 * q + 4, :, :].bitcast(I32), in_=wd_scales.bitcast(I32).rearrange("g q n -> q g n")[4 * q : 4 * q + 4])

        def widen_v(dst, src, cols, g, blocks=(0, 1, 2, 3)):
            for q in blocks:
                o = dst[:, 512 * g : 512 * (g + 1)].rearrange("p (u w e) -> p w u e", u=2, e=2)[:, 32 * q : 32 * q + 32]
                i = src[:, 512 * g + 128 * q : 512 * g + 128 * (q + 1)].bitcast(FP8).rearrange("p (w u e) -> p w u e", u=2, e=2)
                nc.vector.tensor_scalar(out=o, in0=i, scalar1=cols[:, 4 * g + q : 4 * g + q + 1], scalar2=None, op0=ALU.mult)

        def widen_s(dst, src, cols, g, blocks=(0, 1, 2, 3)):
            for q in blocks:
                c = slice(512 * g + 128 * q, 512 * g + 128 * (q + 1))
                nc.scalar.activation(out=dst[:, c], in_=src[:, c].bitcast(FP8), func=ACT.Copy, scale=cols[:, 4 * g + q : 4 * g + q + 1])

        def transposes(bank, wide, on_s):
            words = wide[:].bitcast(F32)
            for g in range(2):
                for u in range(2):
                    if g in on_s:
                        src = words[:, 256 * g + u : 256 * (g + 1) : 2]
                    else:
                        src = words[:, 256 * g + 128 * u : 256 * g + 128 * (u + 1)]
                    nc.tensor.transpose(bank[:, g, u, :], src, ident[:])

        def exit_copy(copy, dst, bank):
            copy(out=dst, in_=bank[:].rearrange("p g u r -> p g r u"))

        wide = {}
        on_s = {}

        def unit_src(i, w):
            g, t = i // 4, i % 4
            return w_raw[(g, w, t // 2)][:, t % 2, :], w_cols[:, w, g, :]

        def alloc_wide(key, halves_on_s):
            wide[key] = work.tile([P, K], BF16, tag="wide", bufs=8, name="wide_t")
            on_s[key] = halves_on_s

        def t_unit(key, tag):
            bank = psum.tile([P, 2, 2, P], F32, tag=tag, name="bank_t")
            transposes(bank, wide.pop(key), on_s[key])
            return bank

        xe = keep.tile([P, 2, T, 4], BF16, align_bytes=64, name="xe")
        xq = keep.tile([P, 2, T], U32, align_bytes=64, name="xq")
        xqs = keep.tile([P, 2, T], U8, align_bytes=64, name="xqs")
        hq = [keep.tile([P, T], U32, align_bytes=64, name=f"hq{g}") for g in range(GROUPS)]
        hqs = [keep.tile([P, T], U8, align_bytes=64, name=f"hqs{g}") for g in range(GROUPS)]

        def x_unit_exit(a, bank, copy):
            dst = xe[:, :, P * a : P * (a + 1), :].rearrange("p g r e -> p g (r e)").bitcast(F32).rearrange("p g (r u) -> p g r u", u=2)
            exit_copy(copy, dst, bank)

        def x_quant(g, h):
            c = slice(256 * h, 256 * (h + 1))
            nc.vector.quantize_mx(out=xq[:, g, c].bitcast(FP8X4), scales=xqs[:, g, c], in_=xe[:, g, c, :].rearrange("p r e -> p (r e)"))

        def w_v(i, w, halves):
            src, cols = unit_src(i, w)
            for g in halves:
                widen_v(wide[(i, w)], src, cols, g)

        def w_s(i, w, halves):
            src, cols = unit_src(i, w)
            for g in halves:
                widen_s(wide[(i, w)], src, cols, g)

        S_COUNT = SCOUNT

        def s_halves(i, w):
            return (1,) if w >= 2 - S_COUNT[i] else ()

        def v_halves(i, w):
            return tuple(g for g in range(2) if g not in s_halves(i, w))

        ew, cw, cws, hm, sil, pa, pb = {}, {}, {}, {}, {}, {}, {}

        def e_unit(i, w, copy, bank):
            if i not in ew:
                ew[i] = work.tile([P, 2, 2, P, 4], BF16, tag="ew", bufs=3, align_bytes=64, name="ew_t")
            dst = ew[i][:, w].rearrange("p g r e -> p g (r e)").bitcast(F32).rearrange("p g (r u) -> p g r u", u=2)
            exit_copy(copy, dst, bank)

        def q_pair(i, parts):
            if i not in cw:
                cw[i] = work.tile([P, 2, 2, P], U32, tag="cw", bufs=3, align_bytes=64, name="cw_t")
                cws[i] = work.tile([P, 2, 2, P], U8, tag="cws", bufs=3, align_bytes=64, name="cws_t")
            for s in parts:
                nc.vector.quantize_mx(
                    out=cw[i][:, s].rearrange("p w g m -> p (w g m)").bitcast(FP8X4),
                    scales=cws[i][:, s].rearrange("p w g m -> p (w g m)"),
                    in_=ew[i][:, s].rearrange("p w g r e -> p (w g r e)"),
                )

        def m_half(i, w):
            (pa, pb)[w][i] = psum.tile([P, T], F32, tag=("a0", "b0")[w], name="pm_t")
            for g in range(2):
                nc.tensor.matmul_mx(
                    out=(pa, pb)[w][i][:], lhsT=cw[i][:, w, g, :].bitcast(FP8X4), lhsT_scale=cws[i][:, w, g, :],
                    rhs=xq[:, g, :].bitcast(FP8X4), rhs_scale=xqs[:, g, :], start=(g == 0), stop=(g == 1),
                )

        def a_pair(i, cuts):
            sil[i] = work.tile([P, T], F32, tag="sil", bufs=3, name="sil_t")
            for c in cuts:
                nc.scalar.activation(out=sil[i][:, c], in_=pa[i][:, c], func=ACT.Silu)

        def b_pair(i, cuts):
            g, t = i // 4, i % 4
            if t == 0:
                hm[g] = work.tile([P, 4, T], BF16, tag="hm", bufs=2, name="hm_t")
            for c in cuts:
                nc.vector.scalar_tensor_tensor(out=hm[g][:, t, c], in0=pb[i][:, c], scalar=sm[:, g, t : t + 1], in1=sil[i][:, c], op0=ALU.mult, op1=ALU.mult)

        hi = {}

        def i_chunk(g, c0, c1, copy):
            if g not in hi:
                hi[g] = work.tile([P, T, 4], BF16, tag="hi", bufs=2, align_bytes=64, name="hi_t")
            dst = hi[g][:, c0:c1, :].rearrange("p (c i) t -> p c t i", i=4)
            src = hm[g][:, :, c0:c1].rearrange("p t (c i) -> p c t i", i=4)
            copy(out=dst, in_=src)

        def qh_chunk(g, c0, c1):
            nc.vector.quantize_mx(out=hq[g][:, c0:c1].bitcast(FP8X4), scales=hqs[g][:, c0:c1], in_=hi[g][:, c0:c1, :].rearrange("p r e -> p (r e)"))

        ybank = {}

        def y_alloc(a, tags):
            for n in range(2):
                ybank[(a, n)] = psum.tile([P, 512], F32, tag=tags[n], name="y_t")

        def y_half(a, n, g):
            nc.tensor.matmul_mx(
                out=ybank[(a, n)][:], lhsT=hq[g][:, P * a : P * (a + 1)].bitcast(FP8X4), lhsT_scale=hqs[g][:, P * a : P * (a + 1)],
                rhs=wd_codes[:, g, 1024 * n : 1024 * (n + 1)].bitcast(FP4X4), rhs_scale=wd_planes[:, g, 512 * n : 512 * (n + 1)],
                start=(g == 0), stop=(g == 3),
            )

        def y_pass(a, g):
            for n in range(2):
                y_half(a, n, g)

        ov = out.rearrange("(p a) n -> p a n", a=4)

        def y_exit(a):
            for n, copy in ((0, nc.scalar.copy), (1, nc.vector.tensor_copy)):
                yt = work.tile([P, 512], F32, tag="yt", bufs=8, name="yt_t")
                copy(out=yt[:], in_=ybank[(a, n)][:])
                nc.sync.dma_start(out=ov[:, a, 512 * n : 512 * (n + 1)], in_=yt[:])

        def y_exit_last():
            for n in range(2):
                for h, copy in ((0, nc.scalar.copy), (1, nc.vector.tensor_copy)):
                    yt = work.tile([P, 256], F32, tag="yl", bufs=4, name="yl_t")
                    copy(out=yt[:], in_=ybank[(3, n)][:, 256 * h : 256 * (h + 1)])
                    nc.sync.dma_start(out=ov[:, 3, 512 * n + 256 * h : 512 * n + 256 * (h + 1)], in_=yt[:])

        WHOLE = (slice(0, T),)
        HALVES = (slice(0, 256), slice(256, 512))
        BOTH = (slice(0, 2),)

        with tc.manual_schedule(engines={mybir.EngineType.PE, mybir.EngineType.Activation, mybir.EngineType.DVE}):
            for a in range(4):
                alloc_wide(("x", a), (1,))
            xcol = lambda a: xs_col[:, a, :]
            warm = keep.tile([P, 1], F32, name="warm")
            nc.scalar.activation(out=warm[:], in_=ident[:, 0:1], func=ACT.Silu)
            spread(0)
            spread(1)
            for a in range(4):
                widen_v(wide[("x", a)], x_raw[a], xcol(a), 0)
                widen_s(wide[("x", a)], x_raw[a], xcol(a), 1)
            pick_cols(nc.vector.tensor_copy)
            xb = [t_unit(("x", a), ("t0", "t1", "a0", "b0")[a]) for a in range(4)]
            for w in range(2):
                alloc_wide((0, w), s_halves(0, w))
            w_v(0, 0, v_halves(0, 0))
            w_v(0, 1, v_halves(0, 1))
            x_unit_exit(0, xb[0], nc.vector.tensor_copy)
            x_unit_exit(1, xb[1], nc.vector.tensor_copy)
            w_s(0, 0, s_halves(0, 0))
            w_s(0, 1, s_halves(0, 1))
            x_unit_exit(2, xb[2], nc.scalar.copy)
            x_unit_exit(3, xb[3], nc.scalar.copy)
            for w in range(2):
                e_unit(0, w, nc.scalar.copy, t_unit((0, w), f"t{w}"))
            for h in range(2):
                for g in range(2):
                    x_quant(g, h)
            for w in range(2):
                alloc_wide((1, w), s_halves(1, w))
                w_s(1, w, s_halves(1, w))
                w_v(1, w, v_halves(1, w))

            y_alloc(0, ("y0", "y1"))
            y_alloc(1, ("y2", "y3"))
            LAST = PAIRS - 1
            banks = {}

            def op_q(s):
                q_pair(s, BOTH if s < LAST else (slice(0, 1), slice(1, 2)))

            def v_list(i):
                return [(w, g, b) for w in range(2) for g in v_halves(i, w) for b in range(4)]

            def s_list(i):
                return [(w, g, b) for w in range(2) for g in s_halves(i, w) for b in range(4)]

            def op_w(s, lo, hi):
                if s + 2 < PAIRS:
                    for w, g, b in v_list(s + 2)[lo:hi]:
                        src, cols = unit_src(s + 2, w)
                        widen_v(wide[(s + 2, w)], src, cols, g, (b,))

            def op_ws(s, lo, hi):
                if s + 2 < PAIRS:
                    for w, g, b in s_list(s + 2)[lo:hi]:
                        src, cols = unit_src(s + 2, w)
                        widen_s(wide[(s + 2, w)], src, cols, g, (b,))

            def op_alloc(s):
                if s + 2 < PAIRS:
                    for w in range(2):
                        alloc_wide((s + 2, w), s_halves(s + 2, w))

            def op_t(s, w):
                if s + 1 < PAIRS:
                    banks[w] = t_unit((s + 1, w), f"t{w}")

            def op_e(s, w):
                if s + 1 < PAIRS:
                    e_unit(s + 1, w, nc.vector.tensor_copy if w == 1 and s + 1 == LAST else nc.scalar.copy, banks[w])

            def op_b(s):
                if s >= 1:
                    b_pair(s - 1, WHOLE)

            def op_m(s, w):
                m_half(s, w)

            def op_i(s, v):
                if s >= 4:
                    g, c = (s - 4) // 4, (s - 4) % 4
                    if c < 2:
                        k = 2 * c + v
                        i_chunk(g, P * k, P * (k + 1), nc.vector.tensor_copy if v else nc.scalar.copy)

            def op_qh(s):
                if 7 <= s < 14 and s % 4 == 3:
                    qh_chunk(s // 4 - 1, 0, 512)
                if s == 14:
                    qh_chunk(2, 0, 512)

            def op_y(s):
                if s >= 8 and s % 4 < 2 and s < 14:
                    y_pass(s % 4, s // 4 - 2)
                if s == LAST:
                    y_pass(0, 2)

            def op_a(s):
                a_pair(s, WHOLE if s < LAST else HALVES)

            OPS = {
                "Q": op_q, "Wa": lambda s: op_w(s, 0, NA), "Wb": lambda s: op_w(s, NA, NB), "Wc": lambda s: op_w(s, NB, 16),
                "Sa": lambda s: op_ws(s, 0, NSA), "Sb": lambda s: op_ws(s, NSA, 16),
                "T0": lambda s: op_t(s, 0), "T1": lambda s: op_t(s, 1), "E0": lambda s: op_e(s, 0), "E1": lambda s: op_e(s, 1),
                "B": op_b, "Ma": lambda s: op_m(s, 0), "Mb": lambda s: op_m(s, 1), "IS": lambda s: op_i(s, 0), "IV": lambda s: op_i(s, 1),
                "QH": op_qh, "Y": op_y, "A": op_a,
            }
            for s in range(PAIRS):
                op_alloc(s)
                for o in ORDER:
                    OPS[o](s)
            y_alloc(2, ("t0", "t1"))
            y_pass(1, 2)
            for g in range(3):
                y_pass(2, g)
            b_pair(LAST, HALVES)
            y_alloc(3, ("a0", "b0"))
            y_pass(3, 0)
            i_chunk(3, 0, 128, nc.vector.tensor_copy)
            i_chunk(3, 128, 256, nc.scalar.copy)
            i_chunk(3, 256, 384, nc.vector.tensor_copy)
            qh_chunk(3, 0, 128)
            y_pass(0, 3)
            i_chunk(3, 384, 512, nc.scalar.copy)
            qh_chunk(3, 128, 256)
            y_pass(1, 3)
            qh_chunk(3, 256, 384)
            y_pass(2, 3)
            qh_chunk(3, 384, 512)
            for n in range(2):
                for g in range(1, 4):
                    y_half(3, n, g)
            for a in range(3):
                y_exit(a)
            y_exit_last()
